import numpy as np
import ml_dtypes


def mxq(x, axis, fmt="e4m3"):
    dtype, down = {"e4m3": (ml_dtypes.float8_e4m3fn, 7), "e5m2": (ml_dtypes.float8_e5m2, 14)}[fmt]
    v = np.moveaxis(np.asarray(x, np.float32).astype(ml_dtypes.bfloat16).astype(np.float64), axis, -1)
    blocks = v.reshape(v.shape[:-1] + (-1, 32))
    amax = np.abs(blocks).max(-1, keepdims=True)
    byte = np.maximum(np.where(amax > 0, np.frexp(amax)[1] - 1 + 127, 0) - down, 1)
    scale = np.exp2(byte - 127.0)
    codes = (blocks / scale).astype(np.float32).astype(dtype).astype(np.float64)
    return np.moveaxis((codes * scale).reshape(v.shape), -1, axis)


WIDE = False


def mx_kscale(k, group=512):
    if not WIDE:
        return np.ones(k)
    levels = np.array([18, -18])
    if group != 512:
        return np.exp2(np.random.permutation(np.resize(levels, k // group))).repeat(group)
    if k % 512:
        return np.exp2(np.random.permutation(np.resize(levels, k // 32))).repeat(32)
    a = np.empty((k // 512, 16))
    for p in range(k // 512):
        a[p, :8] = np.random.permutation(np.resize(levels, 8))
        for g in range(8):
            far = levels[np.abs(levels - a[p, g]) >= 10]
            a[p, g + 8] = far[np.random.randint(len(far))]
    return np.exp2(a.ravel()).repeat(32)


def f64(x):
    return np.asarray(x).astype(np.float64)


def softplus(v):
    return np.log(1.0 + np.exp(v))


G, D, M, O, N = 4, 128, 128, 128, 512


def sgn(shape):
    return np.random.uniform(0.5, 2.0, shape) * np.where(np.random.standard_normal(shape) < 0, -1.0, 1.0)


def setup_inputs():
    n = np.random.standard_normal
    s_d = mx_kscale(D, 0)
    s_m = mx_kscale(M, 0)
    return {
        "x": (n((G, D, N)) * s_d[:, None]).astype(np.float32),
        "w1": (n((G, D, M)) / np.sqrt(D) / s_d[:, None]).astype(np.float32),
        "w2": (n((G, D, M)) / np.sqrt(D) / s_d[:, None]).astype(np.float32),
        "hp1": (np.random.uniform(0.3, 1.0, (G, M, 1))).astype(np.float32),
        "hs": (sgn((G, M, 1)) * s_m[:, None]).astype(np.float32),
        "wo2": (n((G, M, O)) / np.sqrt(M) / s_m[:, None]).astype(np.float32),
        "res": (0.5 * n((G, O, N))).astype(np.float32),
    }


def reference(x, w1, w2, hp1, hs, wo2, res):
    w1q = mxq(f64(w1), 1, "e4m3")
    xq = mxq(f64(x), 1, "e4m3")
    z1 = w1q.transpose(0, 2, 1) @ xq
    w2q = mxq(f64(w2), 1, "e4m3")
    z2 = w2q.transpose(0, 2, 1) @ xq
    q1 = np.square(softplus(z1))
    h = q1 / (q1 + softplus(z2) + f64(hp1)) * 2.0
    hh = h * f64(hs)
    wo2q = mxq(f64(wo2), 1, "e4m3")
    hhq = mxq(hh, 1, "e4m3")
    y0 = wo2q.transpose(0, 2, 1) @ hhq
    y = y0 + f64(res)
    return y

@@ -1,0 +1,199 @@
+from contextlib import ExitStack
+
+import concourse.mybir as mybir
+
+G, D, M, O, N = 4, 128, 128, 128, 512
+FLOPS = 3 * 2 * G * D * M * N
+
+F32 = mybir.dt.float32
+BF16 = mybir.dt.bfloat16
+U32 = mybir.dt.uint32
+U8 = mybir.dt.uint8
+FP8X4 = mybir.dt.float8_e4m3fn_x4
+ACT = mybir.ActivationFunctionType
+ALU = mybir.AluOpType
+
+P = 128
+PACK = 4
+ROWS = 32
+HALF = N // 2
+CHUNK = 128
+EXP_CAP = 2.0**60
+X_SPLIT = 176
+SQUARES_ON_VECTOR = (5, 6, 7)
+
+
+def tile_rows_fhill_kernel(tc, x, w1, w2, hp1, hs, wo2, res, out):
+    nc = tc.nc
+    with ExitStack() as ctx:
+        sb = ctx.enter_context(tc.tile_pool(name="sb", bufs=1))
+        ps = ctx.enter_context(tc.psum_pool(name="ps", bufs=1))
+        ctx.enter_context(tc.manual_schedule())
+
+        def packed_rows(t):
+            return t.rearrange("g (p j) c -> (g p) j c", j=PACK)
+
+        def interleaved(t):
+            return t.rearrange("p j c -> p c j")
+
+        def flat(t):
+            return t.rearrange("p c j -> p (c j)")
+
+        def tile_rows(g):
+            return slice(ROWS * g, ROWS * (g + 1))
+
+        w_raw = [sb.tile([P, PACK, M], F32, name="w_raw%d" % i) for i in range(2)]
+        x_raw = [sb.tile([P, PACK, HALF], F32, name="x_raw%d" % h) for h in range(2)]
+        wo_raw = sb.tile([P, PACK, O], F32)
+        hp_sb = sb.tile([P, G], F32)
+        hs_sb = sb.tile([P, PACK], F32)
+        res_sb = sb.tile([P, G, N], F32)
+        nc.sync.dma_start(out=x_raw[0][:], in_=packed_rows(x)[:, :, :HALF])
+        nc.sync.dma_start(out=w_raw[0][:], in_=packed_rows(w1))
+        nc.sync.dma_start(out=w_raw[1][:], in_=packed_rows(w2))
+        nc.sync.dma_start(out=x_raw[1][:], in_=packed_rows(x)[:, :, HALF:])
+        nc.sync.dma_start(out=wo_raw[:], in_=packed_rows(wo2))
+        with nc.allow_non_contiguous_dma(reason="one half point to a partition"):
+            nc.sync.dma_start(out=hp_sb[:], in_=hp1.rearrange("g m o -> m (g o)"))
+        nc.sync.dma_start(out=hs_sb[:], in_=hs.rearrange("g (p j) o -> (g p) (j o)", j=PACK))
+        nc.sync.dma_start(out=res_sb[:], in_=res.rearrange("g o n -> o g n"))
+
+        w_bf = [sb.tile([P, M, PACK], BF16, align_bytes=64, name="w_bf%d" % i) for i in range(2)]
+        w_codes = [sb.tile([P, M], U32, align_bytes=64, name="w_codes%d" % i) for i in range(2)]
+        w_scales = [sb.tile([P, M], U8, align_bytes=64, name="w_scales%d" % i) for i in range(2)]
+        x_bf = [sb.tile([P, HALF, PACK], BF16, align_bytes=64, name="x_bf%d" % h) for h in range(2)]
+        x_codes = [sb.tile([P, HALF], U32, align_bytes=64, name="x_codes%d" % h) for h in range(2)]
+        x_scales = [sb.tile([P, HALF], U8, align_bytes=64, name="x_scales%d" % h) for h in range(2)]
+        bank = [[ps.tile([P, 2 * HALF], F32, name="bank%d_%d" % (g, h)) for h in range(2)] for g in range(G)]
+
+        def quantise_x(h):
+            nc.vector.quantize_mx(out=x_codes[h][:].bitcast(FP8X4), scales=x_scales[h][:], in_=flat(x_bf[h][:]))
+
+        def quantise_w(i):
+            nc.vector.quantize_mx(out=w_codes[i][:].bitcast(FP8X4), scales=w_scales[i][:], in_=flat(w_bf[i][:]))
+
+        def first_product(h, g, i):
+            for c0 in range(0, HALF, CHUNK):
+                nc.tensor.matmul_mx(
+                    out=bank[g][h][:, i * HALF + c0 : i * HALF + c0 + CHUNK],
+                    lhsT=w_codes[i][tile_rows(g), :].bitcast(FP8X4),
+                    lhsT_scale=w_scales[i][tile_rows(g), :],
+                    rhs=x_codes[h][tile_rows(g), c0 : c0 + CHUNK].bitcast(FP8X4),
+                    rhs_scale=x_scales[h][tile_rows(g), c0 : c0 + CHUNK],
+                    start=True,
+                    stop=True,
+                )
+
+        nc.vector.tensor_copy(out=x_bf[0][:, :X_SPLIT, :], in_=interleaved(x_raw[0][:, :, :X_SPLIT]))
+        nc.scalar.copy(out=x_bf[0][:, X_SPLIT:, :], in_=interleaved(x_raw[0][:, :, X_SPLIT:]))
+        nc.scalar.copy(out=w_bf[0][:], in_=interleaved(w_raw[0][:]))
+        quantise_x(0)
+        nc.vector.tensor_copy(out=w_bf[1][:], in_=interleaved(w_raw[1][:]))
+        quantise_w(0)
+        quantise_w(1)
+        for i in range(2):
+            for g in range(G):
+                first_product(0, g, i)
+        nc.vector.tensor_copy(out=x_bf[1][:], in_=interleaved(x_raw[1][:]))
+        quantise_x(1)
+        for g in range(G):
+            for i in range(2):
+                first_product(1, g, i)
+
+        units = [(h, g) for h in range(2) for g in range(G)]
+        ez = [sb.tile([P, 2 * HALF], F32, name="ez%d" % u) for u in range(len(units))]
+        wo_bf = sb.tile([P, O, PACK], BF16, align_bytes=64)
+        wo_codes = sb.tile([P, O], U32, align_bytes=64)
+        wo_scales = sb.tile([P, O], U8, align_bytes=64)
+        hs2 = sb.tile([P, PACK], F32)
+        nc.vector.tensor_copy(out=wo_bf[:], in_=interleaved(wo_raw[:]))
+        nc.vector.tensor_scalar(out=hs2[:], in0=hs_sb[:], scalar1=2.0, scalar2=None, op0=ALU.mult)
+        nc.vector.quantize_mx(out=wo_codes[:].bitcast(FP8X4), scales=wo_scales[:], in_=flat(wo_bf[:]))
+        for u, (h, g) in enumerate(units):
+            nc.scalar.activation(out=ez[u][:], in_=bank[g][h][:], func=ACT.Exp)
+            nc.vector.tensor_scalar(out=ez[u][:], in0=ez[u][:], scalar1=EXP_CAP, scalar2=None, op0=ALU.min)
+
+        lg = [sb.tile([P, 2 * HALF], F32, name="lg%d" % u) for u in range(len(units))]
+        sp = [sb.tile([P, 2 * HALF], F32, name="sp%d" % u) for u in range(len(units))]
+        q1 = [sb.tile([P, HALF], F32, name="q1%d" % u) for u in range(len(units))]
+        den = [sb.tile([P, HALF], F32, name="den%d" % u) for u in range(len(units))]
+        lden = [sb.tile([P, HALF], F32, name="lden%d" % u) for u in range(len(units))]
+        q1_rows = [sb.tile([P, PACK, HALF], F32, name="q1_rows%d" % h) for h in range(2)]
+        lden_rows = [sb.tile([P, PACK, HALF], F32, name="lden_rows%d" % h) for h in range(2)]
+
+        def log_stage(u):
+            nc.scalar.activation(out=lg[u][:], in_=ez[u][:], func=ACT.Ln, bias=1.0)
+
+        def softplus_stage(u):
+            h, g = units[u]
+            nc.vector.tensor_tensor(out=sp[u][:], in0=bank[g][h][:], in1=lg[u][:], op=ALU.max)
+
+        def square_stage(u):
+            h, g = units[u]
+            if u in SQUARES_ON_VECTOR:
+                nc.vector.tensor_tensor(out=q1[u][:], in0=sp[u][:, :HALF], in1=sp[u][:, :HALF], op=ALU.mult)
+            else:
+                nc.scalar.activation(out=q1[u][:], in_=sp[u][:, :HALF], func=ACT.Square)
+            nc.sync.dma_start(out=q1_rows[h][tile_rows(g), :, :], in_=q1[u][:])
+
+        def sum_stage(u):
+            nc.vector.tensor_tensor(out=den[u][:], in0=q1[u][:], in1=sp[u][:, HALF:], op=ALU.add)
+
+        def logden_stage(u):
+            h, g = units[u]
+            nc.scalar.activation(out=lden[u][:], in_=den[u][:], func=ACT.Ln, bias=hp_sb[:, g : g + 1])
+            nc.sync.dma_start(out=lden_rows[h][tile_rows(g), :, :], in_=lden[u][:])
+
+        stages = [log_stage, softplus_stage, square_stage, sum_stage, logden_stage]
+        for step in range(len(units) + len(stages) - 1):
+            for k in range(len(stages)):
+                if 0 <= step - k < len(units):
+                    stages[k](step - k)
+
+        num = [sb.tile([P, HALF, PACK], F32, name="num%d" % h) for h in range(2)]
+        chunks = N // CHUNK
+        rec = [sb.tile([P, CHUNK, PACK], F32, name="rec%d" % c) for c in range(chunks)]
+        hh_bf = [sb.tile([P, CHUNK, PACK], BF16, align_bytes=64, name="hh_bf%d" % c) for c in range(chunks)]
+        hh_codes = [sb.tile([P, CHUNK], U32, align_bytes=64, name="hh_codes%d" % c) for c in range(chunks)]
+        hh_scales = [sb.tile([P, CHUNK], U8, align_bytes=64, name="hh_scales%d" % c) for c in range(chunks)]
+        y_sb = [sb.tile([P, G, CHUNK], F32, name="y_sb%d" % c) for c in range(chunks)]
+
+        def numerator(h):
+            nc.vector.tensor_tensor(
+                out=num[h][:],
+                in0=interleaved(q1_rows[h][:]),
+                in1=hs2[:].unsqueeze(1).to_broadcast([P, HALF, PACK]),
+                op=ALU.mult,
+            )
+
+        def quotient(c):
+            h, c0 = divmod(c * CHUNK, HALF)
+            nc.scalar.activation(out=rec[c][:], in_=interleaved(lden_rows[h][:, :, c0 : c0 + CHUNK]), func=ACT.Exp, scale=-1.0)
+            nc.vector.tensor_tensor(out=hh_bf[c][:], in0=num[h][:, c0 : c0 + CHUNK, :], in1=rec[c][:], op=ALU.mult)
+
+        def second_product(c):
+            nc.vector.quantize_mx(out=hh_codes[c][:].bitcast(FP8X4), scales=hh_scales[c][:], in_=flat(hh_bf[c][:]))
+            for g in range(G):
+                nc.tensor.matmul_mx(
+                    out=bank[g][c % 2][:, :CHUNK],
+                    lhsT=wo_codes[tile_rows(g), :].bitcast(FP8X4),
+                    lhsT_scale=wo_scales[tile_rows(g), :],
+                    rhs=hh_codes[c][tile_rows(g), :].bitcast(FP8X4),
+                    rhs_scale=hh_scales[c][tile_rows(g), :],
+                    start=True,
+                    stop=True,
+                )
+
+        def residual(c):
+            cols = slice(c * CHUNK, (c + 1) * CHUNK)
+            for g in range(G):
+                nc.vector.tensor_tensor(out=y_sb[c][:, g, :], in0=bank[g][c % 2][:, :CHUNK], in1=res_sb[:, g, cols], op=ALU.add)
+            nc.sync.dma_start(out=out.rearrange("g o n -> o g n")[:, :, cols], in_=y_sb[c][:])
+
+        numerator(0)
+        numerator(1)
+        tail = [quotient, second_product, residual]
+        for step in range(chunks + len(tail) - 1):
+            for k in range(len(tail)):
+                if 0 <= step - k < chunks:
+                    tail[k](step - k)

@@ -20,6 +20,7 @@ HALF = N // 2
 CHUNK = 128
 EXP_CAP = 2.0**60
 X_SPLIT = 176
+RUN = 4
 SQUARES_ON_VECTOR = (5, 6, 7)
 
 
@@ -33,8 +34,11 @@ def tile_rows_fhill_kernel(tc, x, w1, w2, hp1, hs, wo2, res, out):
         def packed_rows(t):
             return t.rearrange("g (p j) c -> (g p) j c", j=PACK)
 
-        def interleaved(t):
-            return t.rearrange("p j c -> p c j")
+        def rows_walk(t):
+            return t.rearrange("p j (c i) -> p c j i", i=RUN)
+
+        def words_walk(t):
+            return t.rearrange("p (c i) j -> p c j i", i=RUN)
 
         def flat(t):
             return t.rearrange("p c j -> p (c j)")
@@ -53,9 +57,9 @@ def tile_rows_fhill_kernel(tc, x, w1, w2, hp1, hs, wo2, res, out):
         nc.sync.dma_start(out=w_raw[1][:], in_=packed_rows(w2))
         nc.sync.dma_start(out=x_raw[1][:], in_=packed_rows(x)[:, :, HALF:])
         nc.sync.dma_start(out=wo_raw[:], in_=packed_rows(wo2))
+        nc.sync.dma_start(out=hs_sb[:], in_=hs.rearrange("g (p j) o -> (g p) (j o)", j=PACK))
         with nc.allow_non_contiguous_dma(reason="one half point to a partition"):
             nc.sync.dma_start(out=hp_sb[:], in_=hp1.rearrange("g m o -> m (g o)"))
-        nc.sync.dma_start(out=hs_sb[:], in_=hs.rearrange("g (p j) o -> (g p) (j o)", j=PACK))
         nc.sync.dma_start(out=res_sb[:], in_=res.rearrange("g o n -> o g n"))
 
         w_bf = [sb.tile([P, M, PACK], BF16, align_bytes=64, name="w_bf%d" % i) for i in range(2)]
@@ -72,8 +76,8 @@ def tile_rows_fhill_kernel(tc, x, w1, w2, hp1, hs, wo2, res, out):
         def quantise_w(i):
             nc.vector.quantize_mx(out=w_codes[i][:].bitcast(FP8X4), scales=w_scales[i][:], in_=flat(w_bf[i][:]))
 
-        def first_product(h, g, i):
-            for c0 in range(0, HALF, CHUNK):
+        def first_product(h, i, c0):
+            for g in range(G):
                 nc.tensor.matmul_mx(
                     out=bank[g][h][:, i * HALF + c0 : i * HALF + c0 + CHUNK],
                     lhsT=w_codes[i][tile_rows(g), :].bitcast(FP8X4),
@@ -84,34 +88,33 @@ def tile_rows_fhill_kernel(tc, x, w1, w2, hp1, hs, wo2, res, out):
                     stop=True,
                 )
 
-        nc.vector.tensor_copy(out=x_bf[0][:, :X_SPLIT, :], in_=interleaved(x_raw[0][:, :, :X_SPLIT]))
-        nc.scalar.copy(out=x_bf[0][:, X_SPLIT:, :], in_=interleaved(x_raw[0][:, :, X_SPLIT:]))
-        nc.scalar.copy(out=w_bf[0][:], in_=interleaved(w_raw[0][:]))
+        def first_products(h):
+            for i in range(2):
+                for c0 in range(0, HALF, CHUNK):
+                    first_product(h, i, c0)
+
+        nc.vector.tensor_copy(out=words_walk(x_bf[0][:, :X_SPLIT, :]), in_=rows_walk(x_raw[0][:, :, :X_SPLIT]))
+        nc.scalar.copy(out=words_walk(x_bf[0][:, X_SPLIT:, :]), in_=rows_walk(x_raw[0][:, :, X_SPLIT:]))
+        nc.scalar.copy(out=words_walk(w_bf[0][:]), in_=rows_walk(w_raw[0][:]))
         quantise_x(0)
-        nc.vector.tensor_copy(out=w_bf[1][:], in_=interleaved(w_raw[1][:]))
+        nc.vector.tensor_copy(out=words_walk(w_bf[1][:]), in_=rows_walk(w_raw[1][:]))
         quantise_w(0)
         quantise_w(1)
-        for i in range(2):
-            for g in range(G):
-                first_product(0, g, i)
-        nc.vector.tensor_copy(out=x_bf[1][:], in_=interleaved(x_raw[1][:]))
+        first_products(0)
+        nc.vector.tensor_copy(out=words_walk(x_bf[1][:]), in_=rows_walk(x_raw[1][:]))
         quantise_x(1)
-        for g in range(G):
-            for i in range(2):
-                first_product(1, g, i)
+        first_products(1)
 
         units = [(h, g) for h in range(2) for g in range(G)]
         ez = [sb.tile([P, 2 * HALF], F32, name="ez%d" % u) for u in range(len(units))]
         wo_bf = sb.tile([P, O, PACK], BF16, align_bytes=64)
         wo_codes = sb.tile([P, O], U32, align_bytes=64)
         wo_scales = sb.tile([P, O], U8, align_bytes=64)
-        hs2 = sb.tile([P, PACK], F32)
-        nc.vector.tensor_copy(out=wo_bf[:], in_=interleaved(wo_raw[:]))
-        nc.vector.tensor_scalar(out=hs2[:], in0=hs_sb[:], scalar1=2.0, scalar2=None, op0=ALU.mult)
-        nc.vector.quantize_mx(out=wo_codes[:].bitcast(FP8X4), scales=wo_scales[:], in_=flat(wo_bf[:]))
+        nc.vector.tensor_copy(out=words_walk(wo_bf[:]), in_=rows_walk(wo_raw[:]))
         for u, (h, g) in enumerate(units):
             nc.scalar.activation(out=ez[u][:], in_=bank[g][h][:], func=ACT.Exp)
             nc.vector.tensor_scalar(out=ez[u][:], in0=ez[u][:], scalar1=EXP_CAP, scalar2=None, op0=ALU.min)
+        nc.vector.quantize_mx(out=wo_codes[:].bitcast(FP8X4), scales=wo_scales[:], in_=flat(wo_bf[:]))
 
         lg = [sb.tile([P, 2 * HALF], F32, name="lg%d" % u) for u in range(len(units))]
         sp = [sb.tile([P, 2 * HALF], F32, name="sp%d" % u) for u in range(len(units))]
@@ -150,26 +153,31 @@ def tile_rows_fhill_kernel(tc, x, w1, w2, hp1, hs, wo2, res, out):
                 if 0 <= step - k < len(units):
                     stages[k](step - k)
 
-        num = [sb.tile([P, HALF, PACK], F32, name="num%d" % h) for h in range(2)]
+        num = [sb.tile([P, PACK, HALF], F32, name="num%d" % h) for h in range(2)]
         chunks = N // CHUNK
-        rec = [sb.tile([P, CHUNK, PACK], F32, name="rec%d" % c) for c in range(chunks)]
+        rec = [sb.tile([P, PACK, CHUNK], F32, name="rec%d" % c) for c in range(chunks)]
+        hh_rows = [sb.tile([P, PACK, CHUNK], BF16, name="hh_rows%d" % c) for c in range(chunks)]
         hh_bf = [sb.tile([P, CHUNK, PACK], BF16, align_bytes=64, name="hh_bf%d" % c) for c in range(chunks)]
         hh_codes = [sb.tile([P, CHUNK], U32, align_bytes=64, name="hh_codes%d" % c) for c in range(chunks)]
         hh_scales = [sb.tile([P, CHUNK], U8, align_bytes=64, name="hh_scales%d" % c) for c in range(chunks)]
         y_sb = [sb.tile([P, G, CHUNK], F32, name="y_sb%d" % c) for c in range(chunks)]
 
         def numerator(h):
-            nc.vector.tensor_tensor(
-                out=num[h][:],
-                in0=interleaved(q1_rows[h][:]),
-                in1=hs2[:].unsqueeze(1).to_broadcast([P, HALF, PACK]),
-                op=ALU.mult,
-            )
+            for j in range(PACK):
+                nc.vector.tensor_scalar(
+                    out=num[h][:, j, :], in0=q1_rows[h][:, j, :], scalar1=hs_sb[:, j : j + 1], scalar2=2.0, op0=ALU.mult, op1=ALU.mult
+                )
+
+        def inverse(c):
+            h, c0 = divmod(c * CHUNK, HALF)
+            nc.scalar.activation(out=rec[c][:], in_=lden_rows[h][:, :, c0 : c0 + CHUNK], func=ACT.Exp, scale=-1.0)
 
         def quotient(c):
             h, c0 = divmod(c * CHUNK, HALF)
-            nc.scalar.activation(out=rec[c][:], in_=interleaved(lden_rows[h][:, :, c0 : c0 + CHUNK]), func=ACT.Exp, scale=-1.0)
-            nc.vector.tensor_tensor(out=hh_bf[c][:], in0=num[h][:, c0 : c0 + CHUNK, :], in1=rec[c][:], op=ALU.mult)
+            nc.vector.tensor_tensor(out=hh_rows[c][:], in0=num[h][:, :, c0 : c0 + CHUNK], in1=rec[c][:], op=ALU.mult)
+
+        def interleave(c, copy):
+            copy(out=words_walk(hh_bf[c][:]), in_=rows_walk(hh_rows[c][:]))
 
         def second_product(c):
             nc.vector.quantize_mx(out=hh_codes[c][:].bitcast(FP8X4), scales=hh_scales[c][:], in_=flat(hh_bf[c][:]))
@@ -192,8 +200,21 @@ def tile_rows_fhill_kernel(tc, x, w1, w2, hp1, hs, wo2, res, out):
 
         numerator(0)
         numerator(1)
-        tail = [quotient, second_product, residual]
-        for step in range(chunks + len(tail) - 1):
-            for k in range(len(tail)):
-                if 0 <= step - k < chunks:
-                    tail[k](step - k)
+        for c in range(chunks):
+            inverse(c)
+        quotient(0)
+        quotient(1)
+        interleave(0, nc.vector.tensor_copy)
+        interleave(1, nc.scalar.copy)
+        quotient(2)
+        interleave(2, nc.scalar.copy)
+        second_product(0)
+        quotient(3)
+        interleave(3, nc.scalar.copy)
+        second_product(1)
+        residual(0)
+        second_product(2)
+        residual(1)
+        second_product(3)
+        residual(2)
+        residual(3)

@@ -51,6 +51,7 @@ def tile_rows_fhill_kernel(tc, x, w1, w2, hp1, hs, wo2, res, out):
         wo_raw = sb.tile([P, PACK, O], F32)
         hp_sb = sb.tile([P, G], F32)
         hs_sb = sb.tile([P, PACK], F32)
+        hs_cols = sb.tile([P, G], F32)
         res_sb = sb.tile([P, G, N], F32)
         nc.sync.dma_start(out=x_raw[0][:], in_=packed_rows(x)[:, :, :HALF])
         nc.sync.dma_start(out=w_raw[0][:], in_=packed_rows(w1))
@@ -60,6 +61,7 @@ def tile_rows_fhill_kernel(tc, x, w1, w2, hp1, hs, wo2, res, out):
         nc.sync.dma_start(out=hs_sb[:], in_=hs.rearrange("g (p j) o -> (g p) (j o)", j=PACK))
         with nc.allow_non_contiguous_dma(reason="one half point to a partition"):
             nc.sync.dma_start(out=hp_sb[:], in_=hp1.rearrange("g m o -> m (g o)"))
+            nc.sync.dma_start(out=hs_cols[:], in_=hs.rearrange("g m o -> m (g o)"))
         nc.sync.dma_start(out=res_sb[:], in_=res.rearrange("g o n -> o g n"))
 
         w_bf = [sb.tile([P, M, PACK], BF16, align_bytes=64, name="w_bf%d" % i) for i in range(2)]
@@ -76,8 +78,8 @@ def tile_rows_fhill_kernel(tc, x, w1, w2, hp1, hs, wo2, res, out):
         def quantise_w(i):
             nc.vector.quantize_mx(out=w_codes[i][:].bitcast(FP8X4), scales=w_scales[i][:], in_=flat(w_bf[i][:]))
 
-        def first_product(h, i, c0):
-            for g in range(G):
+        def first_product(h, i, c0, groups):
+            for g in groups:
                 nc.tensor.matmul_mx(
                     out=bank[g][h][:, i * HALF + c0 : i * HALF + c0 + CHUNK],
                     lhsT=w_codes[i][tile_rows(g), :].bitcast(FP8X4),
@@ -89,9 +91,10 @@ def tile_rows_fhill_kernel(tc, x, w1, w2, hp1, hs, wo2, res, out):
                 )
 
         def first_products(h):
-            for i in range(2):
-                for c0 in range(0, HALF, CHUNK):
-                    first_product(h, i, c0)
+            for g0 in range(0, G, 2):
+                for i in range(2):
+                    for c0 in range(0, HALF, CHUNK):
+                        first_product(h, i, c0, (g0, g0 + 1))
 
         nc.vector.tensor_copy(out=words_walk(x_bf[0][:, :X_SPLIT, :]), in_=rows_walk(x_raw[0][:, :, :X_SPLIT]))
         nc.scalar.copy(out=words_walk(x_bf[0][:, X_SPLIT:, :]), in_=rows_walk(x_raw[0][:, :, X_SPLIT:]))
@@ -114,15 +117,19 @@ def tile_rows_fhill_kernel(tc, x, w1, w2, hp1, hs, wo2, res, out):
         for u, (h, g) in enumerate(units):
             nc.scalar.activation(out=ez[u][:], in_=bank[g][h][:], func=ACT.Exp)
             nc.vector.tensor_scalar(out=ez[u][:], in0=ez[u][:], scalar1=EXP_CAP, scalar2=None, op0=ALU.min)
+        hs2 = sb.tile([P, PACK], F32)
+        nc.vector.tensor_scalar(out=hs2[:], in0=hs_sb[:], scalar1=2.0, scalar2=None, op0=ALU.mult)
+        hs2_cols = sb.tile([P, G], F32)
+        nc.vector.tensor_scalar(out=hs2_cols[:], in0=hs_cols[:], scalar1=2.0, scalar2=None, op0=ALU.mult)
         nc.vector.quantize_mx(out=wo_codes[:].bitcast(FP8X4), scales=wo_scales[:], in_=flat(wo_bf[:]))
 
         lg = [sb.tile([P, 2 * HALF], F32, name="lg%d" % u) for u in range(len(units))]
         sp = [sb.tile([P, 2 * HALF], F32, name="sp%d" % u) for u in range(len(units))]
         q1 = [sb.tile([P, HALF], F32, name="q1%d" % u) for u in range(len(units))]
-        den = [sb.tile([P, HALF], F32, name="den%d" % u) for u in range(len(units))]
         lden = [sb.tile([P, HALF], F32, name="lden%d" % u) for u in range(len(units))]
-        q1_rows = [sb.tile([P, PACK, HALF], F32, name="q1_rows%d" % h) for h in range(2)]
-        lden_rows = [sb.tile([P, PACK, HALF], F32, name="lden_rows%d" % h) for h in range(2)]
+        den = [sb.tile([P, HALF], F32, name="den%d" % u) for u in range(len(units))]
+        q1_rows = sb.tile([P, PACK, HALF], F32)
+        lden_rows = sb.tile([P, PACK, HALF], F32)
 
         def log_stage(u):
             nc.scalar.activation(out=lg[u][:], in_=ez[u][:], func=ACT.Ln, bias=1.0)
@@ -137,7 +144,8 @@ def tile_rows_fhill_kernel(tc, x, w1, w2, hp1, hs, wo2, res, out):
                 nc.vector.tensor_tensor(out=q1[u][:], in0=sp[u][:, :HALF], in1=sp[u][:, :HALF], op=ALU.mult)
             else:
                 nc.scalar.activation(out=q1[u][:], in_=sp[u][:, :HALF], func=ACT.Square)
-            nc.sync.dma_start(out=q1_rows[h][tile_rows(g), :, :], in_=q1[u][:])
+            if h == 0:
+                nc.sync.dma_start(out=q1_rows[tile_rows(g), :, :], in_=q1[u][:])
 
         def sum_stage(u):
             nc.vector.tensor_tensor(out=den[u][:], in0=q1[u][:], in1=sp[u][:, HALF:], op=ALU.add)
@@ -145,7 +153,8 @@ def tile_rows_fhill_kernel(tc, x, w1, w2, hp1, hs, wo2, res, out):
         def logden_stage(u):
             h, g = units[u]
             nc.scalar.activation(out=lden[u][:], in_=den[u][:], func=ACT.Ln, bias=hp_sb[:, g : g + 1])
-            nc.sync.dma_start(out=lden_rows[h][tile_rows(g), :, :], in_=lden[u][:])
+            if h == 0:
+                nc.sync.dma_start(out=lden_rows[tile_rows(g), :, :], in_=lden[u][:])
 
         stages = [log_stage, softplus_stage, square_stage, sum_stage, logden_stage]
         for step in range(len(units) + len(stages) - 1):
@@ -153,31 +162,40 @@ def tile_rows_fhill_kernel(tc, x, w1, w2, hp1, hs, wo2, res, out):
                 if 0 <= step - k < len(units):
                     stages[k](step - k)
 
-        num = [sb.tile([P, PACK, HALF], F32, name="num%d" % h) for h in range(2)]
         chunks = N // CHUNK
-        rec = [sb.tile([P, PACK, CHUNK], F32, name="rec%d" % c) for c in range(chunks)]
-        hh_rows = [sb.tile([P, PACK, CHUNK], BF16, name="hh_rows%d" % c) for c in range(chunks)]
+        rec = [sb.tile([P, PACK, CHUNK], F32, name="rec%d" % c) for c in range(chunks // 2)]
+        hh_early = [sb.tile([P, PACK, CHUNK], BF16, name="hh_early%d" % c) for c in range(chunks // 2)]
+        hh_late = sb.tile([P, PACK, HALF], BF16)
+        hh_rows = [hh_early[0][:], hh_early[1][:], hh_late[:, :, :CHUNK], hh_late[:, :, CHUNK:]]
+        rec_cols = [sb.tile([P, HALF], F32, name="rec_cols%d" % g) for g in range(G)]
+        hh_cols = [sb.tile([P, HALF], BF16, name="hh_cols%d" % g) for g in range(G)]
         hh_bf = [sb.tile([P, CHUNK, PACK], BF16, align_bytes=64, name="hh_bf%d" % c) for c in range(chunks)]
         hh_codes = [sb.tile([P, CHUNK], U32, align_bytes=64, name="hh_codes%d" % c) for c in range(chunks)]
         hh_scales = [sb.tile([P, CHUNK], U8, align_bytes=64, name="hh_scales%d" % c) for c in range(chunks)]
         y_sb = [sb.tile([P, G, CHUNK], F32, name="y_sb%d" % c) for c in range(chunks)]
 
-        def numerator(h):
+        def late_quotient(g):
+            nc.scalar.activation(out=rec_cols[g][:], in_=lden[G + g][:], func=ACT.Exp, scale=-1.0)
+            nc.vector.scalar_tensor_tensor(
+                out=hh_cols[g][:], in0=q1[G + g][:], scalar=hs2_cols[:, g : g + 1], in1=rec_cols[g][:], op0=ALU.mult, op1=ALU.mult
+            )
+            nc.sync.dma_start(out=hh_late[tile_rows(g), :, :], in_=hh_cols[g][:])
+
+        def early_quotient(c):
+            c0 = c * CHUNK
+            nc.scalar.activation(out=rec[c][:], in_=lden_rows[:, :, c0 : c0 + CHUNK], func=ACT.Exp, scale=-1.0)
             for j in range(PACK):
-                nc.vector.tensor_scalar(
-                    out=num[h][:, j, :], in0=q1_rows[h][:, j, :], scalar1=hs_sb[:, j : j + 1], scalar2=2.0, op0=ALU.mult, op1=ALU.mult
+                nc.vector.scalar_tensor_tensor(
+                    out=hh_early[c][:, j, :],
+                    in0=q1_rows[:, j, c0 : c0 + CHUNK],
+                    scalar=hs2[:, j : j + 1],
+                    in1=rec[c][:, j, :],
+                    op0=ALU.mult,
+                    op1=ALU.mult,
                 )
 
-        def inverse(c):
-            h, c0 = divmod(c * CHUNK, HALF)
-            nc.scalar.activation(out=rec[c][:], in_=lden_rows[h][:, :, c0 : c0 + CHUNK], func=ACT.Exp, scale=-1.0)
-
-        def quotient(c):
-            h, c0 = divmod(c * CHUNK, HALF)
-            nc.vector.tensor_tensor(out=hh_rows[c][:], in0=num[h][:, :, c0 : c0 + CHUNK], in1=rec[c][:], op=ALU.mult)
-
         def interleave(c, copy):
-            copy(out=words_walk(hh_bf[c][:]), in_=rows_walk(hh_rows[c][:]))
+            copy(out=words_walk(hh_bf[c][:]), in_=rows_walk(hh_rows[c]))
 
         def second_product(c):
             nc.vector.quantize_mx(out=hh_codes[c][:].bitcast(FP8X4), scales=hh_scales[c][:], in_=flat(hh_bf[c][:]))
@@ -196,23 +214,23 @@ def tile_rows_fhill_kernel(tc, x, w1, w2, hp1, hs, wo2, res, out):
             cols = slice(c * CHUNK, (c + 1) * CHUNK)
             for g in range(G):
                 nc.vector.tensor_tensor(out=y_sb[c][:, g, :], in0=bank[g][c % 2][:, :CHUNK], in1=res_sb[:, g, cols], op=ALU.add)
-            nc.sync.dma_start(out=out.rearrange("g o n -> o g n")[:, :, cols], in_=y_sb[c][:])
+                if c == chunks - 1 and g % 2 == 1:
+                    queue = nc.sync if g == 1 else nc.scalar
+                    queue.dma_start(out=out.rearrange("g o n -> o g n")[:, g - 1 : g + 1, cols], in_=y_sb[c][:, g - 1 : g + 1, :])
+            if c < chunks - 1:
+                nc.sync.dma_start(out=out.rearrange("g o n -> o g n")[:, :, cols], in_=y_sb[c][:])
 
-        numerator(0)
-        numerator(1)
-        for c in range(chunks):
-            inverse(c)
-        quotient(0)
-        quotient(1)
-        interleave(0, nc.vector.tensor_copy)
-        interleave(1, nc.scalar.copy)
-        quotient(2)
-        interleave(2, nc.scalar.copy)
+        for g in range(G):
+            late_quotient(g)
+        early_quotient(0)
+        early_quotient(1)
+        interleave(0, nc.scalar.copy)
         second_product(0)
-        quotient(3)
+        interleave(1, nc.vector.tensor_copy)
+        interleave(2, nc.scalar.copy)
         interleave(3, nc.scalar.copy)
-        second_product(1)
         residual(0)
+        second_product(1)
         second_product(2)
         residual(1)
         second_product(3)

@@ -18,10 +18,14 @@ PACK = 4
 ROWS = 32
 HALF = N // 2
 CHUNK = 128
+EARLY_CHUNKS = (0, 1)
+LATE_CHUNKS = (2, 3)
 EXP_CAP = 2.0**60
-X_SPLIT = 176
 RUN = 4
-SQUARES_ON_VECTOR = (5, 6, 7)
+X_SPLIT = 176
+GROUP_ORDER = (0, 2, 1, 3)
+SQUARES_ON_VECTOR = (0, 7)
+STAGE_LAGS = (0, 1, 2, 3, 6)
 
 
 def tile_rows_fhill_kernel(tc, x, w1, w2, hp1, hs, wo2, res, out):
@@ -31,7 +35,7 @@ def tile_rows_fhill_kernel(tc, x, w1, w2, hp1, hs, wo2, res, out):
         ps = ctx.enter_context(tc.psum_pool(name="ps", bufs=1))
         ctx.enter_context(tc.manual_schedule())
 
-        def packed_rows(t):
+        def hbm_rows(t):
             return t.rearrange("g (p j) c -> (g p) j c", j=PACK)
 
         def rows_walk(t):
@@ -40,8 +44,8 @@ def tile_rows_fhill_kernel(tc, x, w1, w2, hp1, hs, wo2, res, out):
         def words_walk(t):
             return t.rearrange("p (c i) j -> p c j i", i=RUN)
 
-        def flat(t):
-            return t.rearrange("p c j -> p (c j)")
+        def quantise(codes, scales, words):
+            nc.vector.quantize_mx(out=codes[:].bitcast(FP8X4), scales=scales[:], in_=words[:].rearrange("p c j -> p (c j)"))
 
         def tile_rows(g):
             return slice(ROWS * g, ROWS * (g + 1))
@@ -49,18 +53,18 @@ def tile_rows_fhill_kernel(tc, x, w1, w2, hp1, hs, wo2, res, out):
         w_raw = [sb.tile([P, PACK, M], F32, name="w_raw%d" % i) for i in range(2)]
         x_raw = [sb.tile([P, PACK, HALF], F32, name="x_raw%d" % h) for h in range(2)]
         wo_raw = sb.tile([P, PACK, O], F32)
-        hp_sb = sb.tile([P, G], F32)
-        hs_sb = sb.tile([P, PACK], F32)
+        hp_cols = sb.tile([P, G], F32)
+        hs_rows = sb.tile([P, PACK], F32)
         hs_cols = sb.tile([P, G], F32)
         res_sb = sb.tile([P, G, N], F32)
-        nc.sync.dma_start(out=x_raw[0][:], in_=packed_rows(x)[:, :, :HALF])
-        nc.sync.dma_start(out=w_raw[0][:], in_=packed_rows(w1))
-        nc.sync.dma_start(out=w_raw[1][:], in_=packed_rows(w2))
-        nc.sync.dma_start(out=x_raw[1][:], in_=packed_rows(x)[:, :, HALF:])
-        nc.sync.dma_start(out=wo_raw[:], in_=packed_rows(wo2))
-        nc.sync.dma_start(out=hs_sb[:], in_=hs.rearrange("g (p j) o -> (g p) (j o)", j=PACK))
-        with nc.allow_non_contiguous_dma(reason="one half point to a partition"):
-            nc.sync.dma_start(out=hp_sb[:], in_=hp1.rearrange("g m o -> m (g o)"))
+        nc.sync.dma_start(out=x_raw[0][:], in_=hbm_rows(x)[:, :, :HALF])
+        nc.sync.dma_start(out=w_raw[0][:], in_=hbm_rows(w1))
+        nc.sync.dma_start(out=w_raw[1][:], in_=hbm_rows(w2))
+        nc.sync.dma_start(out=x_raw[1][:], in_=hbm_rows(x)[:, :, HALF:])
+        nc.sync.dma_start(out=wo_raw[:], in_=hbm_rows(wo2))
+        nc.sync.dma_start(out=hs_rows[:], in_=hs.rearrange("g (p j) o -> (g p) (j o)", j=PACK))
+        with nc.allow_non_contiguous_dma(reason="one value of each group to a partition"):
+            nc.sync.dma_start(out=hp_cols[:], in_=hp1.rearrange("g m o -> m (g o)"))
             nc.sync.dma_start(out=hs_cols[:], in_=hs.rearrange("g m o -> m (g o)"))
         nc.sync.dma_start(out=res_sb[:], in_=res.rearrange("g o n -> o g n"))
 
@@ -72,43 +76,34 @@ def tile_rows_fhill_kernel(tc, x, w1, w2, hp1, hs, wo2, res, out):
         x_scales = [sb.tile([P, HALF], U8, align_bytes=64, name="x_scales%d" % h) for h in range(2)]
         bank = [[ps.tile([P, 2 * HALF], F32, name="bank%d_%d" % (g, h)) for h in range(2)] for g in range(G)]
 
-        def quantise_x(h):
-            nc.vector.quantize_mx(out=x_codes[h][:].bitcast(FP8X4), scales=x_scales[h][:], in_=flat(x_bf[h][:]))
-
-        def quantise_w(i):
-            nc.vector.quantize_mx(out=w_codes[i][:].bitcast(FP8X4), scales=w_scales[i][:], in_=flat(w_bf[i][:]))
-
-        def first_product(h, i, c0, groups):
-            for g in groups:
-                nc.tensor.matmul_mx(
-                    out=bank[g][h][:, i * HALF + c0 : i * HALF + c0 + CHUNK],
-                    lhsT=w_codes[i][tile_rows(g), :].bitcast(FP8X4),
-                    lhsT_scale=w_scales[i][tile_rows(g), :],
-                    rhs=x_codes[h][tile_rows(g), c0 : c0 + CHUNK].bitcast(FP8X4),
-                    rhs_scale=x_scales[h][tile_rows(g), c0 : c0 + CHUNK],
-                    start=True,
-                    stop=True,
-                )
-
         def first_products(h):
-            for g0 in range(0, G, 2):
+            for first in range(0, G, 2):
                 for i in range(2):
                     for c0 in range(0, HALF, CHUNK):
-                        first_product(h, i, c0, (g0, g0 + 1))
+                        for g in GROUP_ORDER[first : first + 2]:
+                            nc.tensor.matmul_mx(
+                                out=bank[g][h][:, i * HALF + c0 : i * HALF + c0 + CHUNK],
+                                lhsT=w_codes[i][tile_rows(g), :].bitcast(FP8X4),
+                                lhsT_scale=w_scales[i][tile_rows(g), :],
+                                rhs=x_codes[h][tile_rows(g), c0 : c0 + CHUNK].bitcast(FP8X4),
+                                rhs_scale=x_scales[h][tile_rows(g), c0 : c0 + CHUNK],
+                                start=True,
+                                stop=True,
+                            )
 
         nc.vector.tensor_copy(out=words_walk(x_bf[0][:, :X_SPLIT, :]), in_=rows_walk(x_raw[0][:, :, :X_SPLIT]))
         nc.scalar.copy(out=words_walk(x_bf[0][:, X_SPLIT:, :]), in_=rows_walk(x_raw[0][:, :, X_SPLIT:]))
         nc.scalar.copy(out=words_walk(w_bf[0][:]), in_=rows_walk(w_raw[0][:]))
-        quantise_x(0)
+        quantise(x_codes[0], x_scales[0], x_bf[0])
         nc.vector.tensor_copy(out=words_walk(w_bf[1][:]), in_=rows_walk(w_raw[1][:]))
-        quantise_w(0)
-        quantise_w(1)
+        for i in range(2):
+            quantise(w_codes[i], w_scales[i], w_bf[i])
         first_products(0)
         nc.vector.tensor_copy(out=words_walk(x_bf[1][:]), in_=rows_walk(x_raw[1][:]))
-        quantise_x(1)
+        quantise(x_codes[1], x_scales[1], x_bf[1])
         first_products(1)
 
-        units = [(h, g) for h in range(2) for g in range(G)]
+        units = [(h, g) for h in range(2) for g in GROUP_ORDER]
         ez = [sb.tile([P, 2 * HALF], F32, name="ez%d" % u) for u in range(len(units))]
         wo_bf = sb.tile([P, O, PACK], BF16, align_bytes=64)
         wo_codes = sb.tile([P, O], U32, align_bytes=64)
@@ -117,17 +112,13 @@ def tile_rows_fhill_kernel(tc, x, w1, w2, hp1, hs, wo2, res, out):
         for u, (h, g) in enumerate(units):
             nc.scalar.activation(out=ez[u][:], in_=bank[g][h][:], func=ACT.Exp)
             nc.vector.tensor_scalar(out=ez[u][:], in0=ez[u][:], scalar1=EXP_CAP, scalar2=None, op0=ALU.min)
-        hs2 = sb.tile([P, PACK], F32)
-        nc.vector.tensor_scalar(out=hs2[:], in0=hs_sb[:], scalar1=2.0, scalar2=None, op0=ALU.mult)
-        hs2_cols = sb.tile([P, G], F32)
-        nc.vector.tensor_scalar(out=hs2_cols[:], in0=hs_cols[:], scalar1=2.0, scalar2=None, op0=ALU.mult)
-        nc.vector.quantize_mx(out=wo_codes[:].bitcast(FP8X4), scales=wo_scales[:], in_=flat(wo_bf[:]))
+        quantise(wo_codes, wo_scales, wo_bf)
 
         lg = [sb.tile([P, 2 * HALF], F32, name="lg%d" % u) for u in range(len(units))]
         sp = [sb.tile([P, 2 * HALF], F32, name="sp%d" % u) for u in range(len(units))]
         q1 = [sb.tile([P, HALF], F32, name="q1%d" % u) for u in range(len(units))]
         lden = [sb.tile([P, HALF], F32, name="lden%d" % u) for u in range(len(units))]
-        den = [sb.tile([P, HALF], F32, name="den%d" % u) for u in range(len(units))]
+        part = [sb.tile([P, HALF], F32, name="part%d" % u) for u in range(len(units))]
         q1_rows = sb.tile([P, PACK, HALF], F32)
         lden_rows = sb.tile([P, PACK, HALF], F32)
 
@@ -148,57 +139,57 @@ def tile_rows_fhill_kernel(tc, x, w1, w2, hp1, hs, wo2, res, out):
                 nc.sync.dma_start(out=q1_rows[tile_rows(g), :, :], in_=q1[u][:])
 
         def sum_stage(u):
-            nc.vector.tensor_tensor(out=den[u][:], in0=q1[u][:], in1=sp[u][:, HALF:], op=ALU.add)
+            nc.vector.tensor_tensor(out=part[u][:], in0=q1[u][:], in1=sp[u][:, HALF:], op=ALU.add)
 
-        def logden_stage(u):
+        def log_den_stage(u):
             h, g = units[u]
-            nc.scalar.activation(out=lden[u][:], in_=den[u][:], func=ACT.Ln, bias=hp_sb[:, g : g + 1])
+            nc.scalar.activation(out=lden[u][:], in_=part[u][:], func=ACT.Ln, bias=hp_cols[:, g : g + 1])
             if h == 0:
                 nc.sync.dma_start(out=lden_rows[tile_rows(g), :, :], in_=lden[u][:])
 
-        stages = [log_stage, softplus_stage, square_stage, sum_stage, logden_stage]
-        for step in range(len(units) + len(stages) - 1):
-            for k in range(len(stages)):
-                if 0 <= step - k < len(units):
-                    stages[k](step - k)
+        stages = [log_stage, softplus_stage, square_stage, sum_stage, log_den_stage]
+        for step in range(len(units) + STAGE_LAGS[-1]):
+            for stage, lag in zip(stages, STAGE_LAGS):
+                if 0 <= step - lag < len(units):
+                    stage(step - lag)
 
         chunks = N // CHUNK
-        rec = [sb.tile([P, PACK, CHUNK], F32, name="rec%d" % c) for c in range(chunks // 2)]
-        hh_early = [sb.tile([P, PACK, CHUNK], BF16, name="hh_early%d" % c) for c in range(chunks // 2)]
-        hh_late = sb.tile([P, PACK, HALF], BF16)
-        hh_rows = [hh_early[0][:], hh_early[1][:], hh_late[:, :, :CHUNK], hh_late[:, :, CHUNK:]]
+        rec_rows = [sb.tile([P, PACK, CHUNK], F32, name="rec_rows%d" % c) for c in EARLY_CHUNKS]
+        hh_rows = {c: sb.tile([P, PACK, CHUNK], BF16, name="hh_rows%d" % c) for c in LATE_CHUNKS}
+        hs2_cols = sb.tile([P, G], F32)
+        num_rows = sb.tile([P, PACK, HALF], F32)
         rec_cols = [sb.tile([P, HALF], F32, name="rec_cols%d" % g) for g in range(G)]
         hh_cols = [sb.tile([P, HALF], BF16, name="hh_cols%d" % g) for g in range(G)]
         hh_bf = [sb.tile([P, CHUNK, PACK], BF16, align_bytes=64, name="hh_bf%d" % c) for c in range(chunks)]
         hh_codes = [sb.tile([P, CHUNK], U32, align_bytes=64, name="hh_codes%d" % c) for c in range(chunks)]
         hh_scales = [sb.tile([P, CHUNK], U8, align_bytes=64, name="hh_scales%d" % c) for c in range(chunks)]
         y_sb = [sb.tile([P, G, CHUNK], F32, name="y_sb%d" % c) for c in range(chunks)]
+        out_view = out.rearrange("g o n -> o g n")
 
-        def late_quotient(g):
-            nc.scalar.activation(out=rec_cols[g][:], in_=lden[G + g][:], func=ACT.Exp, scale=-1.0)
-            nc.vector.scalar_tensor_tensor(
-                out=hh_cols[g][:], in0=q1[G + g][:], scalar=hs2_cols[:, g : g + 1], in1=rec_cols[g][:], op0=ALU.mult, op1=ALU.mult
-            )
-            nc.sync.dma_start(out=hh_late[tile_rows(g), :, :], in_=hh_cols[g][:])
-
-        def early_quotient(c):
-            c0 = c * CHUNK
-            nc.scalar.activation(out=rec[c][:], in_=lden_rows[:, :, c0 : c0 + CHUNK], func=ACT.Exp, scale=-1.0)
-            for j in range(PACK):
+        def late_quotient(c):
+            cols = slice(c * CHUNK - HALF, (c + 1) * CHUNK - HALF)
+            for u in range(G, 2 * G):
+                g = units[u][1]
+                nc.scalar.activation(out=rec_cols[g][:, cols], in_=lden[u][:, cols], func=ACT.Exp, scale=-1.0)
                 nc.vector.scalar_tensor_tensor(
-                    out=hh_early[c][:, j, :],
-                    in0=q1_rows[:, j, c0 : c0 + CHUNK],
-                    scalar=hs2[:, j : j + 1],
-                    in1=rec[c][:, j, :],
+                    out=hh_cols[g][:, cols],
+                    in0=q1[u][:, cols],
+                    scalar=hs2_cols[:, g : g + 1],
+                    in1=rec_cols[g][:, cols],
                     op0=ALU.mult,
                     op1=ALU.mult,
                 )
+                nc.sync.dma_start(out=hh_rows[c][tile_rows(g), :, :], in_=hh_cols[g][:, cols])
 
-        def interleave(c, copy):
-            copy(out=words_walk(hh_bf[c][:]), in_=rows_walk(hh_rows[c]))
+        def early_quotient(c):
+            cols = slice(c * CHUNK, (c + 1) * CHUNK)
+            nc.scalar.activation(out=rec_rows[c][:], in_=lden_rows[:, :, cols], func=ACT.Exp, scale=-1.0)
+            nc.vector.tensor_tensor(
+                out=words_walk(hh_bf[c][:]), in0=rows_walk(num_rows[:, :, cols]), in1=rows_walk(rec_rows[c][:]), op=ALU.mult
+            )
 
         def second_product(c):
-            nc.vector.quantize_mx(out=hh_codes[c][:].bitcast(FP8X4), scales=hh_scales[c][:], in_=flat(hh_bf[c][:]))
+            quantise(hh_codes[c], hh_scales[c], hh_bf[c])
             for g in range(G):
                 nc.tensor.matmul_mx(
                     out=bank[g][c % 2][:, :CHUNK],
@@ -210,29 +201,29 @@ def tile_rows_fhill_kernel(tc, x, w1, w2, hp1, hs, wo2, res, out):
                     stop=True,
                 )
 
-        def residual(c):
+        def add_residual(c, groups, queue):
             cols = slice(c * CHUNK, (c + 1) * CHUNK)
-            for g in range(G):
+            for g in range(groups.start, groups.stop):
                 nc.vector.tensor_tensor(out=y_sb[c][:, g, :], in0=bank[g][c % 2][:, :CHUNK], in1=res_sb[:, g, cols], op=ALU.add)
-                if c == chunks - 1 and g % 2 == 1:
-                    queue = nc.sync if g == 1 else nc.scalar
-                    queue.dma_start(out=out.rearrange("g o n -> o g n")[:, g - 1 : g + 1, cols], in_=y_sb[c][:, g - 1 : g + 1, :])
-            if c < chunks - 1:
-                nc.sync.dma_start(out=out.rearrange("g o n -> o g n")[:, :, cols], in_=y_sb[c][:])
+            queue.dma_start(out=out_view[:, groups, cols], in_=y_sb[c][:, groups, :])
 
-        for g in range(G):
-            late_quotient(g)
-        early_quotient(0)
-        early_quotient(1)
-        interleave(0, nc.scalar.copy)
-        second_product(0)
-        interleave(1, nc.vector.tensor_copy)
-        interleave(2, nc.scalar.copy)
-        interleave(3, nc.scalar.copy)
-        residual(0)
-        second_product(1)
-        second_product(2)
-        residual(1)
-        second_product(3)
-        residual(2)
-        residual(3)
+        nc.vector.tensor_scalar(out=hs2_cols[:], in0=hs_cols[:], scalar1=2.0, scalar2=None, op0=ALU.mult)
+        for j in range(PACK):
+            nc.vector.tensor_scalar(
+                out=num_rows[:, j, :], in0=q1_rows[:, j, :], scalar1=hs_rows[:, j : j + 1], scalar2=2.0, op0=ALU.mult, op1=ALU.mult
+            )
+        for c in LATE_CHUNKS:
+            late_quotient(c)
+        for c in EARLY_CHUNKS:
+            early_quotient(c)
+        for c in LATE_CHUNKS:
+            nc.scalar.copy(out=words_walk(hh_bf[c][:]), in_=rows_walk(hh_rows[c][:]))
+        for c in EARLY_CHUNKS:
+            second_product(c)
+        all_groups = slice(0, G)
+        for c in LATE_CHUNKS:
+            add_residual(c - 2, all_groups, nc.sync)
+            second_product(c)
+        add_residual(LATE_CHUNKS[0], all_groups, nc.sync)
+        add_residual(LATE_CHUNKS[1], slice(0, G // 2), nc.sync)
+        add_residual(LATE_CHUNKS[1], slice(G // 2, G), nc.scalar)

from contextlib import ExitStack

import concourse.mybir as mybir

G, D, M, O, N = 4, 128, 128, 128, 512
FLOPS = 3 * 2 * G * D * M * N

F32 = mybir.dt.float32
BF16 = mybir.dt.bfloat16
U32 = mybir.dt.uint32
U8 = mybir.dt.uint8
FP8X4 = mybir.dt.float8_e4m3fn_x4
ACT = mybir.ActivationFunctionType
ALU = mybir.AluOpType

P = 128
PACK = 4
ROWS = 32
HALF = N // 2
CHUNK = 128
EARLY_CHUNKS = (0, 1)
LATE_CHUNKS = (2, 3)
EXP_CAP = 2.0**60
RUN = 4
X_SPLIT = 176
GROUP_ORDER = (0, 2, 1, 3)
SQUARES_ON_VECTOR = (0, 7)
STAGE_LAGS = (0, 1, 2, 3, 6)


def tile_rows_fhill_kernel(tc, x, w1, w2, hp1, hs, wo2, res, out):
    nc = tc.nc
    with ExitStack() as ctx:
        sb = ctx.enter_context(tc.tile_pool(name="sb", bufs=1))
        ps = ctx.enter_context(tc.psum_pool(name="ps", bufs=1))
        ctx.enter_context(tc.manual_schedule())

        def hbm_rows(t):
            return t.rearrange("g (p j) c -> (g p) j c", j=PACK)

        def rows_walk(t):
            return t.rearrange("p j (c i) -> p c j i", i=RUN)

        def words_walk(t):
            return t.rearrange("p (c i) j -> p c j i", i=RUN)

        def quantise(codes, scales, words):
            nc.vector.quantize_mx(out=codes[:].bitcast(FP8X4), scales=scales[:], in_=words[:].rearrange("p c j -> p (c j)"))

        def tile_rows(g):
            return slice(ROWS * g, ROWS * (g + 1))

        w_raw = [sb.tile([P, PACK, M], F32, name="w_raw%d" % i) for i in range(2)]
        x_raw = [sb.tile([P, PACK, HALF], F32, name="x_raw%d" % h) for h in range(2)]
        wo_raw = sb.tile([P, PACK, O], F32)
        hp_cols = sb.tile([P, G], F32)
        hs_rows = sb.tile([P, PACK], F32)
        hs_cols = sb.tile([P, G], F32)
        res_sb = sb.tile([P, G, N], F32)
        nc.sync.dma_start(out=x_raw[0][:], in_=hbm_rows(x)[:, :, :HALF])
        nc.sync.dma_start(out=w_raw[0][:], in_=hbm_rows(w1))
        nc.sync.dma_start(out=w_raw[1][:], in_=hbm_rows(w2))
        nc.sync.dma_start(out=x_raw[1][:], in_=hbm_rows(x)[:, :, HALF:])
        nc.sync.dma_start(out=wo_raw[:], in_=hbm_rows(wo2))
        nc.sync.dma_start(out=hs_rows[:], in_=hs.rearrange("g (p j) o -> (g p) (j o)", j=PACK))
        with nc.allow_non_contiguous_dma(reason="one value of each group to a partition"):
            nc.sync.dma_start(out=hp_cols[:], in_=hp1.rearrange("g m o -> m (g o)"))
            nc.sync.dma_start(out=hs_cols[:], in_=hs.rearrange("g m o -> m (g o)"))
        nc.sync.dma_start(out=res_sb[:], in_=res.rearrange("g o n -> o g n"))

        w_bf = [sb.tile([P, M, PACK], BF16, align_bytes=64, name="w_bf%d" % i) for i in range(2)]
        w_codes = [sb.tile([P, M], U32, align_bytes=64, name="w_codes%d" % i) for i in range(2)]
        w_scales = [sb.tile([P, M], U8, align_bytes=64, name="w_scales%d" % i) for i in range(2)]
        x_bf = [sb.tile([P, HALF, PACK], BF16, align_bytes=64, name="x_bf%d" % h) for h in range(2)]
        x_codes = [sb.tile([P, HALF], U32, align_bytes=64, name="x_codes%d" % h) for h in range(2)]
        x_scales = [sb.tile([P, HALF], U8, align_bytes=64, name="x_scales%d" % h) for h in range(2)]
        bank = [[ps.tile([P, 2 * HALF], F32, name="bank%d_%d" % (g, h)) for h in range(2)] for g in range(G)]

        def first_products(h):
            for first in range(0, G, 2):
                for i in range(2):
                    for c0 in range(0, HALF, CHUNK):
                        for g in GROUP_ORDER[first : first + 2]:
                            nc.tensor.matmul_mx(
                                out=bank[g][h][:, i * HALF + c0 : i * HALF + c0 + CHUNK],
                                lhsT=w_codes[i][tile_rows(g), :].bitcast(FP8X4),
                                lhsT_scale=w_scales[i][tile_rows(g), :],
                                rhs=x_codes[h][tile_rows(g), c0 : c0 + CHUNK].bitcast(FP8X4),
                                rhs_scale=x_scales[h][tile_rows(g), c0 : c0 + CHUNK],
                                start=True,
                                stop=True,
                            )

        nc.vector.tensor_copy(out=words_walk(x_bf[0][:, :X_SPLIT, :]), in_=rows_walk(x_raw[0][:, :, :X_SPLIT]))
        nc.scalar.copy(out=words_walk(x_bf[0][:, X_SPLIT:, :]), in_=rows_walk(x_raw[0][:, :, X_SPLIT:]))
        nc.scalar.copy(out=words_walk(w_bf[0][:]), in_=rows_walk(w_raw[0][:]))
        quantise(x_codes[0], x_scales[0], x_bf[0])
        nc.vector.tensor_copy(out=words_walk(w_bf[1][:]), in_=rows_walk(w_raw[1][:]))
        for i in range(2):
            quantise(w_codes[i], w_scales[i], w_bf[i])
        first_products(0)
        nc.vector.tensor_copy(out=words_walk(x_bf[1][:]), in_=rows_walk(x_raw[1][:]))
        quantise(x_codes[1], x_scales[1], x_bf[1])
        first_products(1)

        units = [(h, g) for h in range(2) for g in GROUP_ORDER]
        ez = [sb.tile([P, 2 * HALF], F32, name="ez%d" % u) for u in range(len(units))]
        wo_bf = sb.tile([P, O, PACK], BF16, align_bytes=64)
        wo_codes = sb.tile([P, O], U32, align_bytes=64)
        wo_scales = sb.tile([P, O], U8, align_bytes=64)
        nc.vector.tensor_copy(out=words_walk(wo_bf[:]), in_=rows_walk(wo_raw[:]))
        for u, (h, g) in enumerate(units):
            nc.scalar.activation(out=ez[u][:], in_=bank[g][h][:], func=ACT.Exp)
            nc.vector.tensor_scalar(out=ez[u][:], in0=ez[u][:], scalar1=EXP_CAP, scalar2=None, op0=ALU.min)
        quantise(wo_codes, wo_scales, wo_bf)

        lg = [sb.tile([P, 2 * HALF], F32, name="lg%d" % u) for u in range(len(units))]
        sp = [sb.tile([P, 2 * HALF], F32, name="sp%d" % u) for u in range(len(units))]
        q1 = [sb.tile([P, HALF], F32, name="q1%d" % u) for u in range(len(units))]
        lden = [sb.tile([P, HALF], F32, name="lden%d" % u) for u in range(len(units))]
        part = [sb.tile([P, HALF], F32, name="part%d" % u) for u in range(len(units))]
        q1_rows = sb.tile([P, PACK, HALF], F32)
        lden_rows = sb.tile([P, PACK, HALF], F32)

        def log_stage(u):
            nc.scalar.activation(out=lg[u][:], in_=ez[u][:], func=ACT.Ln, bias=1.0)

        def softplus_stage(u):
            h, g = units[u]
            nc.vector.tensor_tensor(out=sp[u][:], in0=bank[g][h][:], in1=lg[u][:], op=ALU.max)

        def square_stage(u):
            h, g = units[u]
            if u in SQUARES_ON_VECTOR:
                nc.vector.tensor_tensor(out=q1[u][:], in0=sp[u][:, :HALF], in1=sp[u][:, :HALF], op=ALU.mult)
            else:
                nc.scalar.activation(out=q1[u][:], in_=sp[u][:, :HALF], func=ACT.Square)
            if h == 0:
                nc.sync.dma_start(out=q1_rows[tile_rows(g), :, :], in_=q1[u][:])

        def sum_stage(u):
            nc.vector.tensor_tensor(out=part[u][:], in0=q1[u][:], in1=sp[u][:, HALF:], op=ALU.add)

        def log_den_stage(u):
            h, g = units[u]
            nc.scalar.activation(out=lden[u][:], in_=part[u][:], func=ACT.Ln, bias=hp_cols[:, g : g + 1])
            if h == 0:
                nc.sync.dma_start(out=lden_rows[tile_rows(g), :, :], in_=lden[u][:])

        stages = [log_stage, softplus_stage, square_stage, sum_stage, log_den_stage]
        for step in range(len(units) + STAGE_LAGS[-1]):
            for stage, lag in zip(stages, STAGE_LAGS):
                if 0 <= step - lag < len(units):
                    stage(step - lag)

        chunks = N // CHUNK
        rec_rows = [sb.tile([P, PACK, CHUNK], F32, name="rec_rows%d" % c) for c in EARLY_CHUNKS]
        hh_rows = {c: sb.tile([P, PACK, CHUNK], BF16, name="hh_rows%d" % c) for c in LATE_CHUNKS}
        hs2_cols = sb.tile([P, G], F32)
        num_rows = sb.tile([P, PACK, HALF], F32)
        rec_cols = [sb.tile([P, HALF], F32, name="rec_cols%d" % g) for g in range(G)]
        hh_cols = [sb.tile([P, HALF], BF16, name="hh_cols%d" % g) for g in range(G)]
        hh_bf = [sb.tile([P, CHUNK, PACK], BF16, align_bytes=64, name="hh_bf%d" % c) for c in range(chunks)]
        hh_codes = [sb.tile([P, CHUNK], U32, align_bytes=64, name="hh_codes%d" % c) for c in range(chunks)]
        hh_scales = [sb.tile([P, CHUNK], U8, align_bytes=64, name="hh_scales%d" % c) for c in range(chunks)]
        y_sb = [sb.tile([P, G, CHUNK], F32, name="y_sb%d" % c) for c in range(chunks)]
        out_view = out.rearrange("g o n -> o g n")

        def late_quotient(c):
            cols = slice(c * CHUNK - HALF, (c + 1) * CHUNK - HALF)
            for u in range(G, 2 * G):
                g = units[u][1]
                nc.scalar.activation(out=rec_cols[g][:, cols], in_=lden[u][:, cols], func=ACT.Exp, scale=-1.0)
                nc.vector.scalar_tensor_tensor(
                    out=hh_cols[g][:, cols],
                    in0=q1[u][:, cols],
                    scalar=hs2_cols[:, g : g + 1],
                    in1=rec_cols[g][:, cols],
                    op0=ALU.mult,
                    op1=ALU.mult,
                )
                nc.sync.dma_start(out=hh_rows[c][tile_rows(g), :, :], in_=hh_cols[g][:, cols])

        def early_quotient(c):
            cols = slice(c * CHUNK, (c + 1) * CHUNK)
            nc.scalar.activation(out=rec_rows[c][:], in_=lden_rows[:, :, cols], func=ACT.Exp, scale=-1.0)
            nc.vector.tensor_tensor(
                out=words_walk(hh_bf[c][:]), in0=rows_walk(num_rows[:, :, cols]), in1=rows_walk(rec_rows[c][:]), op=ALU.mult
            )

        def second_product(c):
            quantise(hh_codes[c], hh_scales[c], hh_bf[c])
            for g in range(G):
                nc.tensor.matmul_mx(
                    out=bank[g][c % 2][:, :CHUNK],
                    lhsT=wo_codes[tile_rows(g), :].bitcast(FP8X4),
                    lhsT_scale=wo_scales[tile_rows(g), :],
                    rhs=hh_codes[c][tile_rows(g), :].bitcast(FP8X4),
                    rhs_scale=hh_scales[c][tile_rows(g), :],
                    start=True,
                    stop=True,
                )

        def add_residual(c, groups, queue):
            cols = slice(c * CHUNK, (c + 1) * CHUNK)
            for g in range(groups.start, groups.stop):
                nc.vector.tensor_tensor(out=y_sb[c][:, g, :], in0=bank[g][c % 2][:, :CHUNK], in1=res_sb[:, g, cols], op=ALU.add)
            queue.dma_start(out=out_view[:, groups, cols], in_=y_sb[c][:, groups, :])

        nc.vector.tensor_scalar(out=hs2_cols[:], in0=hs_cols[:], scalar1=2.0, scalar2=None, op0=ALU.mult)
        for j in range(PACK):
            nc.vector.tensor_scalar(
                out=num_rows[:, j, :], in0=q1_rows[:, j, :], scalar1=hs_rows[:, j : j + 1], scalar2=2.0, op0=ALU.mult, op1=ALU.mult
            )
        for c in LATE_CHUNKS:
            late_quotient(c)
        for c in EARLY_CHUNKS:
            early_quotient(c)
        for c in LATE_CHUNKS:
            nc.scalar.copy(out=words_walk(hh_bf[c][:]), in_=rows_walk(hh_rows[c][:]))
        for c in EARLY_CHUNKS:
            second_product(c)
        all_groups = slice(0, G)
        for c in LATE_CHUNKS:
            add_residual(c - 2, all_groups, nc.sync)
            second_product(c)
        add_residual(LATE_CHUNKS[0], all_groups, nc.sync)
        add_residual(LATE_CHUNKS[1], slice(0, G // 2), nc.sync)
        add_residual(LATE_CHUNKS[1], slice(G // 2, G), nc.scalar)
